import numpy as np
import ml_dtypes


def mxq(x, axis, fmt="e4m3"):
    dtype, down = {"e4m3": (ml_dtypes.float8_e4m3fn, 7), "e5m2": (ml_dtypes.float8_e5m2, 14)}[fmt]
    v = np.moveaxis(np.asarray(x, np.float32).astype(ml_dtypes.bfloat16).astype(np.float64), axis, -1)
    blocks = v.reshape(v.shape[:-1] + (-1, 32))
    amax = np.abs(blocks).max(-1, keepdims=True)
    byte = np.maximum(np.where(amax > 0, np.frexp(amax)[1] - 1 + 127, 0) - down, 1)
    scale = np.exp2(byte - 127.0)
    codes = (blocks / scale).astype(np.float32).astype(dtype).astype(np.float64)
    return np.moveaxis((codes * scale).reshape(v.shape), -1, axis)


WIDE = False


def mx_kscale(k):
    if not WIDE:
        return np.ones(k)
    levels = np.array([10, -10, 5, -5, 0])
    if k % 512:
        return np.exp2(np.random.permutation(np.resize(levels, k // 32))).repeat(32)
    a = np.empty((k // 512, 16))
    for p in range(k // 512):
        a[p, :8] = np.random.permutation(np.resize(levels, 8))
        for g in range(8):
            far = levels[np.abs(levels - a[p, g]) >= 10]
            a[p, g + 8] = far[np.random.randint(len(far))]
    return np.exp2(a.ravel()).repeat(32)


def f64(x):
    return np.asarray(x).astype(np.float64)


def striped(idx):
    return np.tile(idx.reshape(-1, 16).T, (8, 1)).astype(np.uint16)


def unstriped(offs):
    return offs[:16].T.reshape(-1).astype(np.int64)


E2M1 = np.array([0.0, 0.5, 1.0, 1.5, 2.0, 3.0, 4.0, 6.0, -0.0, -0.5, -1.0, -1.5, -2.0, -3.0, -4.0, -6.0])


def pack_weight(w, fmt):
    k, n = w.shape
    w = f64(np.asarray(w, np.float32).astype(ml_dtypes.bfloat16)).reshape(k // 32, 32, n)
    amax = np.abs(w).max(1)
    if fmt == "e4m3":
        byte = np.frexp(amax)[1] - 1 + 127 - 7
    else:
        mant, ex = np.frexp(amax / 6.0)
        byte = np.where(mant > 0.5, ex, ex - 1) + 127
    byte = np.clip(np.where(amax > 0, byte, 1), 1, 254)
    scaled = (w * np.exp2(127.0 - byte)[:, None, :]).reshape(k, n).astype(np.float32)
    by_word = np.ascontiguousarray(scaled.reshape(k // 512, 128, 4, n).transpose(0, 1, 3, 2))
    if fmt == "e4m3":
        words = by_word.astype(ml_dtypes.float8_e4m3fn).view(np.uint8)
    else:
        c = by_word.astype(ml_dtypes.float4_e2m1fn).view(np.uint8) & 0xF
        words = (c[..., 0::2] | (c[..., 1::2] << 4)).reshape(k // 512, 128, 2 * n)
    return np.ascontiguousarray(words), np.ascontiguousarray(byte.astype(np.uint8).reshape(k // 512, 16, n))


def unpack_weight(words, scales, fmt):
    g, _, n = scales.shape
    words = np.ascontiguousarray(words).reshape(g, 128, n, -1)
    if fmt == "e4m3":
        vals = words.view(ml_dtypes.float8_e4m3fn).astype(np.float64)
    else:
        nib = np.empty((g, 128, n, 4), np.uint8)
        nib[..., 0::2] = words & 0xF
        nib[..., 1::2] = words >> 4
        vals = E2M1[nib]
    vals = vals * np.repeat(np.exp2(scales.astype(np.float64) - 127.0), 8, axis=1)[..., None]
    return vals.transpose(0, 1, 3, 2).reshape(g * 512, n)


def gelu(v):
    return 0.5 * v * (1.0 + np.tanh(np.sqrt(2.0 / np.pi) * (v + 0.044715 * v**3)))


K, T, E, C, H, N = 1024, 640, 15, 128, 512, 128
TOP = 3


def by_expert(wq, xq):
    return np.concatenate([wq[e].T @ xq[:, e * C:(e + 1) * C] for e in range(E)], axis=1)


def setup_inputs():
    n = np.random.standard_normal
    s = mx_kscale(K)[:, None]
    u = mx_kscale(H)
    deal = np.repeat(np.arange(E), C).reshape(TOP, T)[:, np.random.permutation(T)]
    deal = np.take_along_axis(deal, np.argsort(np.random.rand(TOP, T), axis=0), axis=0)
    for _ in range(8):
        s_, t_ = np.random.permutation(T).reshape(2, -1); r = np.random.randint(TOP, size=T // 2); x, y = deal[r, s_].copy(), deal[r, t_].copy()
        ok = ~((deal[:, s_] == y).any(0) | (deal[:, t_] == x).any(0)); deal[r[ok], s_[ok]] = y[ok]; deal[r[ok], t_[ok]] = x[ok]
    order = np.lexsort((np.random.rand(TOP * T), deal.reshape(-1)))
    slot_token = order % T; pos = np.empty(TOP * T, np.int64); pos[order] = np.arange(TOP * T); pos = pos.reshape(TOP, T)
    g = np.random.uniform(0.5, 1.5, (TOP, T)); g = g / g.sum(0)
    x = pack_weight(n((K, T)) * s, "e4m3")
    return {
        "x_words": x[0],
        "x_scales": x[1],
        "w1": (n((E, K, H)) / np.sqrt(K) / s[None] * u[None, None, :]).astype(np.float32),
        "w2": (n((E, H, N)) / np.sqrt(H) / u[None, :, None]).astype(np.float32),
        "gate": np.stack([np.tile(r, (N, 1)) for r in g]).astype(np.float32),
        "offs": striped(slot_token),
        "pos1": striped(pos[0]),
        "pos2": striped(pos[1]),
        "pos3": striped(pos[2]),
    }


def reference(x_words, x_scales, w1, w2, gate, offs, pos1, pos2, pos3):
    idx = unstriped(offs)
    xq = unpack_weight(x_words, x_scales, "e4m3")[:, idx]
    h = gelu(by_expert(mxq(f64(w1), 1, "e4m3"), xq))
    y = by_expert(mxq(f64(w2), 1, "e4m3"), mxq(h, 0, "e4m3"))
    return sum(f64(gate[r]) * y[:, unstriped(p)] for r, p in enumerate((pos1, pos2, pos3)))

@@ -1,0 +1,212 @@
+from contextlib import ExitStack
+
+import concourse.mybir as mybir
+
+K, T, E, C, H, N = 1024, 640, 15, 128, 512, 128
+TOP = 3
+S = E * C
+FLOPS = 2 * S * (K * H + H * N)
+
+F32 = mybir.dt.float32
+BF16 = mybir.dt.bfloat16
+I32 = mybir.dt.int32
+U32 = mybir.dt.uint32
+U16 = mybir.dt.uint16
+U8 = mybir.dt.uint8
+FP8X4 = mybir.dt.float8_e4m3fn_x4
+GELU = mybir.ActivationFunctionType.Gelu_apprx_tanh
+MULT = mybir.AluOpType.mult
+
+P = 128
+PACK = 4
+PASSES = K // (P * PACK)
+STRIPE = 16
+GATHER_EXPERTS = 3
+STREAM_BUFS = 7
+W2_EARLY = {1: (0, 4), 5: (4, 8), 9: (8, 10)}
+W2_LATE = ((10, 12), (12, 14), (14, 15))
+VECTOR_SHARE = 88
+TOKEN_CUTS = (0, 320, 640)
+
+
+def tile_moe_pkd_mlp_gelu_kernel(
+    tc, x_words, x_scales, w1, w2, gate, offs, pos1, pos2, pos3, out
+):
+    nc = tc.nc
+    with ExitStack() as ctx:
+        keep = ctx.enter_context(tc.tile_pool(name="keep", bufs=1))
+        stream = ctx.enter_context(tc.tile_pool(name="stream", bufs=STREAM_BUFS))
+        work = ctx.enter_context(tc.tile_pool(name="work", bufs=3))
+        psum = ctx.enter_context(tc.psum_pool(name="psum", bufs=4))
+
+        tok_scales = keep.tile([P, T], U8, name="tok_scales", align_bytes=64)
+        nc.vector.memset(tok_scales[:].bitcast(I32), 0)
+        warm = keep.tile([P, 8], F32, name="warm")
+        warm_out = keep.tile([P, 8], F32, name="warm_out")
+        nc.vector.memset(warm[:], 0.0)
+        nc.scalar.activation(warm_out[:], warm[:], GELU)
+
+        slot_token = keep.tile([P, S // STRIPE], U16, name="slot_token")
+        nc.sync.dma_start(slot_token[:], offs)
+        tok_words = keep.tile([P, PASSES, T], I32, name="tok_words", align_bytes=64)
+        nc.sync.dma_start(tok_words[:], x_words.rearrange("o p t r -> p o (t r)").bitcast(I32))
+        for q in range(4):
+            nc.sync.dma_start(
+                tok_scales[32 * q : 32 * q + 4 * PASSES, :].bitcast(I32),
+                x_scales[:, 4 * q : 4 * q + 4, :].bitcast(I32),
+            )
+        token_slot = [keep.tile([P, T // STRIPE], U16, name="token_slot%d" % r) for r in range(TOP)]
+
+        h_words = keep.tile([P, S], U32, name="h_words", align_bytes=64)
+        h_scales = keep.tile([P, S], U8, name="h_scales", align_bytes=64)
+        w2_words = keep.tile([P, E * N], U32, name="w2_words", align_bytes=64)
+        w2_scales = keep.tile([P, E * N], U8, name="w2_scales", align_bytes=64)
+        y = keep.tile([P, S], F32, name="y")
+
+        def gather_tokens(e0):
+            slots = slice(e0 * C, (e0 + GATHER_EXPERTS) * C)
+            offsets = slot_token[:, slots.start // STRIPE : slots.stop // STRIPE]
+            words = work.tile([P, PASSES, GATHER_EXPERTS * C], U32, name="slot_words", bufs=2, align_bytes=64)
+            scales = work.tile([P, GATHER_EXPERTS * C], U8, name="slot_scales", bufs=2, align_bytes=64)
+            for o in range(PASSES):
+                nc.vector.tensor_copy(words[:, o, :], tok_words[:, o, :].bitcast(U32).indirect(offsets))
+            nc.vector.tensor_copy(scales[:], tok_scales[:].indirect(offsets))
+            return words, scales
+
+        def load_w1(e):
+            if e < E - 1:
+                raw = stream.tile([P, PASSES, PACK * H], F32, name="w1_raw", tag="stream", align_bytes=64)
+                nc.sync.dma_start(raw[:], w1[e].rearrange("(o p j) i -> p o (j i)", p=P, j=PACK))
+                return [raw[:, o, :] for o in range(PASSES)]
+            raws = []
+            for o in range(PASSES):
+                raw = stream.tile([P, PACK * H], F32, name="w1_raw_pass", tag="stream", align_bytes=64)
+                nc.sync.dma_start(raw[:], w1[e].rearrange("(o p j) i -> o p (j i)", p=P, j=PACK)[o])
+                raws.append(raw[:])
+            return raws
+
+        def round_w1(e, raws):
+            grouped = []
+            for o, raw in enumerate(raws):
+                g = work.tile([P, PACK * H], BF16, name="w1_bf16_%d" % o, align_bytes=64)
+                dst = g[:].rearrange("p (t m j) -> p m j t", t=PACK, j=PACK)
+                src = raw.rearrange("p (j m t) -> p m j t", j=PACK, t=PACK)
+                if e == E - 1:
+                    nc.vector.tensor_copy(dst[:, :VECTOR_SHARE], src[:, :VECTOR_SHARE])
+                    nc.scalar.copy(dst[:, VECTOR_SHARE:], src[:, VECTOR_SHARE:])
+                elif o == 0:
+                    nc.scalar.copy(dst, src)
+                else:
+                    nc.vector.tensor_copy(dst, src)
+                grouped.append(g)
+            return grouped
+
+        def first_layer(e, grouped, slot_words, slot_scales):
+            slots = slice(e % GATHER_EXPERTS * C, (e % GATHER_EXPERTS + 1) * C)
+            codes = []
+            for o in reversed(range(PASSES)) if e < E - 1 else range(PASSES):
+                words = work.tile([P, H], U32, name="w1_words%d" % o, align_bytes=64)
+                scales = work.tile([P, H], U8, name="w1_scales%d" % o, align_bytes=64)
+                nc.vector.quantize_mx(out=words[:].bitcast(FP8X4), scales=scales[:], in_=grouped[o][:])
+                codes.append((o, words, scales))
+            codes = sorted(codes, key=lambda item: item[0])
+            a = psum.tile([P, PACK, C], F32, name="a")
+            for t in range(PACK):
+                cols = slice(t * P, (t + 1) * P)
+                for o, words, scales in codes:
+                    nc.tensor.matmul_mx(
+                        out=a[:, t, :],
+                        lhsT=words[:, cols].bitcast(FP8X4),
+                        lhsT_scale=scales[:, cols],
+                        rhs=slot_words[:, o, slots].bitcast(FP8X4),
+                        rhs_scale=slot_scales[4 * o :, slots],
+                        start=(o == 0),
+                        stop=(o == PASSES - 1),
+                    )
+            return a
+
+        def hidden(e, a, spent):
+            slots = slice(e * C, (e + 1) * C)
+            h = spent[:, : C * PACK // 2].bitcast(BF16)
+            nc.scalar.activation(h.rearrange("p (c t) -> p c t", t=PACK), a[:].rearrange("p t c -> p c t"), GELU)
+            nc.vector.quantize_mx(out=h_words[:, slots].bitcast(FP8X4), scales=h_scales[:, slots], in_=h)
+
+        def load_w2(e0, e1):
+            raw = stream.tile([P, e1 - e0, PACK * N], F32, name="w2_raw", tag="stream", align_bytes=64)
+            nc.sync.dma_start(raw[:], w2[e0:e1].rearrange("e (p j) n -> p e (j n)", j=PACK))
+            return raw
+
+        def quantize_w2(e0, e1, raw, on_vector):
+            g = work.tile([P, (e1 - e0) * N * PACK], BF16, name="w2_bf16", align_bytes=64)
+            for e in range(e1 - e0):
+                dst = g[:, e * N * PACK : (e + 1) * N * PACK].rearrange("p (c i j) -> p c j i", i=4, j=PACK)
+                src = raw[:, e, :].rearrange("p (j c i) -> p c j i", j=PACK, i=4)
+                if on_vector(e0 + e):
+                    nc.vector.tensor_copy(dst, src)
+                else:
+                    nc.scalar.copy(dst, src)
+            cols = slice(e0 * N, e1 * N)
+            nc.vector.quantize_mx(out=w2_words[:, cols].bitcast(FP8X4), scales=w2_scales[:, cols], in_=g[:])
+
+        def second_layer(e0, e1):
+            acc = psum.tile([P, (e1 - e0) * C], F32, name="acc")
+            for e in range(e0, e1):
+                cols = slice(e * N, (e + 1) * N)
+                slots = slice(e * C, (e + 1) * C)
+                nc.tensor.matmul_mx(
+                    out=acc[:, (e - e0) * C : (e - e0 + 1) * C],
+                    lhsT=w2_words[:, cols].bitcast(FP8X4),
+                    lhsT_scale=w2_scales[:, cols],
+                    rhs=h_words[:, slots].bitcast(FP8X4),
+                    rhs_scale=h_scales[:, slots],
+                    start=True,
+                    stop=True,
+                )
+            nc.scalar.copy(y[:, e0 * C : e1 * C], acc[:])
+
+        sums = None
+        for e in range(E):
+            raws = load_w1(e)
+            if e == 1:
+                for lst, pos in zip(token_slot, (pos1, pos2, pos3)):
+                    nc.sync.dma_start(lst[:], pos)
+            if e % GATHER_EXPERTS == 0:
+                tokens = gather_tokens(e)
+            grouped = round_w1(e, raws)
+            previous = sums
+            sums = first_layer(e, grouped, *tokens)
+            if e > 0:
+                hidden(e - 1, previous, raws[0])
+            if e in W2_EARLY:
+                e0, e1 = W2_EARLY[e]
+                quantize_w2(e0, e1, load_w2(e0, e1), lambda x: False)
+            for e0, e1 in W2_EARLY.values():
+                if e == e1:
+                    second_layer(e0, e1)
+        late = [load_w2(e0, e1) for e0, e1 in W2_LATE]
+        gates = []
+        for r in range(TOP):
+            g = stream.tile([P, T], F32, name="gate", tag="stream", align_bytes=64)
+            nc.sync.dma_start(g[:], gate[r])
+            gates.append(g)
+        for (e0, e1), raw in zip(W2_LATE, late):
+            quantize_w2(e0, e1, raw, lambda x: x % 2 == 0)
+            if e1 == E - 1:
+                hidden(E - 1, sums, raw[:, 1, :])
+        second_layer(W2_LATE[0][0], E - 1)
+        second_layer(E - 1, E)
+
+        parts = [keep.tile([P, T], F32, name="part%d" % r) for r in range(TOP)]
+        pair = keep.tile([P, T], F32, name="pair")
+        total = keep.tile([P, T], F32, name="total")
+        for t0, t1 in zip(TOKEN_CUTS, TOKEN_CUTS[1:]):
+            for r in range(TOP):
+                nc.vector.tensor_tensor(
+                    parts[r][:, t0:t1],
+                    y[:].indirect(token_slot[r][:, t0 // STRIPE : t1 // STRIPE]),
+                    gates[r][:, t0:t1],
+                    MULT,
+                )
+            nc.vector.tensor_add(pair[:, t0:t1], parts[0][:, t0:t1], parts[1][:, t0:t1])
+            nc.vector.tensor_add(total[:, t0:t1], pair[:, t0:t1], parts[2][:, t0:t1])
+            nc.sync.dma_start(out[:, t0:t1], total[:, t0:t1])

@@ -25,8 +25,8 @@ GATHER_EXPERTS = 3
 STREAM_BUFS = 7
 W2_EARLY = {1: (0, 4), 5: (4, 8), 9: (8, 10)}
 W2_LATE = ((10, 12), (12, 14), (14, 15))
-VECTOR_SHARE = 88
-TOKEN_CUTS = (0, 320, 640)
+VECTOR_SHARE = (52, 88)
+TOKEN_CUT = 384
 
 
 def tile_moe_pkd_mlp_gelu_kernel(
@@ -47,9 +47,9 @@ def tile_moe_pkd_mlp_gelu_kernel(
         nc.scalar.activation(warm_out[:], warm[:], GELU)
 
         slot_token = keep.tile([P, S // STRIPE], U16, name="slot_token")
-        nc.sync.dma_start(slot_token[:], offs)
         tok_words = keep.tile([P, PASSES, T], I32, name="tok_words", align_bytes=64)
         nc.sync.dma_start(tok_words[:], x_words.rearrange("o p t r -> p o (t r)").bitcast(I32))
+        nc.sync.dma_start(slot_token[:], offs)
         for q in range(4):
             nc.sync.dma_start(
                 tok_scales[32 * q : 32 * q + 4 * PASSES, :].bitcast(I32),
@@ -57,10 +57,10 @@ def tile_moe_pkd_mlp_gelu_kernel(
             )
         token_slot = [keep.tile([P, T // STRIPE], U16, name="token_slot%d" % r) for r in range(TOP)]
 
-        h_words = keep.tile([P, S], U32, name="h_words", align_bytes=64)
-        h_scales = keep.tile([P, S], U8, name="h_scales", align_bytes=64)
-        w2_words = keep.tile([P, E * N], U32, name="w2_words", align_bytes=64)
-        w2_scales = keep.tile([P, E * N], U8, name="w2_scales", align_bytes=64)
+        h_words = keep.tile([P, S - C], U32, name="h_words", align_bytes=64)
+        h_scales = keep.tile([P, S - C], U8, name="h_scales", align_bytes=64)
+        w2_words = keep.tile([P, (E - 1) * N], U32, name="w2_words", align_bytes=64)
+        w2_scales = keep.tile([P, (E - 1) * N], U8, name="w2_scales", align_bytes=64)
         y = keep.tile([P, S], F32, name="y")
 
         def gather_tokens(e0):
@@ -74,7 +74,7 @@ def tile_moe_pkd_mlp_gelu_kernel(
             return words, scales
 
         def load_w1(e):
-            if e < E - 1:
+            if e < E - 2:
                 raw = stream.tile([P, PASSES, PACK * H], F32, name="w1_raw", tag="stream", align_bytes=64)
                 nc.sync.dma_start(raw[:], w1[e].rearrange("(o p j) i -> p o (j i)", p=P, j=PACK))
                 return [raw[:, o, :] for o in range(PASSES)]
@@ -92,8 +92,9 @@ def tile_moe_pkd_mlp_gelu_kernel(
                 dst = g[:].rearrange("p (t m j) -> p m j t", t=PACK, j=PACK)
                 src = raw.rearrange("p (j m t) -> p m j t", j=PACK, t=PACK)
                 if e == E - 1:
-                    nc.vector.tensor_copy(dst[:, :VECTOR_SHARE], src[:, :VECTOR_SHARE])
-                    nc.scalar.copy(dst[:, VECTOR_SHARE:], src[:, VECTOR_SHARE:])
+                    cut = VECTOR_SHARE[o]
+                    nc.vector.tensor_copy(dst[:, :cut], src[:, :cut])
+                    nc.scalar.copy(dst[:, cut:], src[:, cut:])
                 elif o == 0:
                     nc.scalar.copy(dst, src)
                 else:
@@ -104,10 +105,16 @@ def tile_moe_pkd_mlp_gelu_kernel(
         def first_layer(e, grouped, slot_words, slot_scales):
             slots = slice(e % GATHER_EXPERTS * C, (e % GATHER_EXPERTS + 1) * C)
             codes = []
-            for o in reversed(range(PASSES)) if e < E - 1 else range(PASSES):
+            for o in reversed(range(PASSES)) if e < E - 2 else range(PASSES):
                 words = work.tile([P, H], U32, name="w1_words%d" % o, align_bytes=64)
                 scales = work.tile([P, H], U8, name="w1_scales%d" % o, align_bytes=64)
-                nc.vector.quantize_mx(out=words[:].bitcast(FP8X4), scales=scales[:], in_=grouped[o][:])
+                step = P if (e, o) == (E - 1, PASSES - 1) else H
+                for c in range(0, H, step):
+                    nc.vector.quantize_mx(
+                        out=words[:, c : c + step].bitcast(FP8X4),
+                        scales=scales[:, c : c + step],
+                        in_=grouped[o][:, PACK * c : PACK * (c + step)],
+                    )
                 codes.append((o, words, scales))
             codes = sorted(codes, key=lambda item: item[0])
             a = psum.tile([P, PACK, C], F32, name="a")
@@ -136,15 +143,18 @@ def tile_moe_pkd_mlp_gelu_kernel(
             nc.sync.dma_start(raw[:], w2[e0:e1].rearrange("e (p j) n -> p e (j n)", j=PACK))
             return raw
 
+        def round_w2(grouped, raw, on_vector):
+            dst = grouped.rearrange("p (c i j) -> p c j i", i=4, j=PACK)
+            src = raw.rearrange("p (j c i) -> p c j i", j=PACK, i=4)
+            if on_vector:
+                nc.vector.tensor_copy(dst, src)
+            else:
+                nc.scalar.copy(dst, src)
+
         def quantize_w2(e0, e1, raw, on_vector):
             g = work.tile([P, (e1 - e0) * N * PACK], BF16, name="w2_bf16", align_bytes=64)
             for e in range(e1 - e0):
-                dst = g[:, e * N * PACK : (e + 1) * N * PACK].rearrange("p (c i j) -> p c j i", i=4, j=PACK)
-                src = raw[:, e, :].rearrange("p (j c i) -> p c j i", j=PACK, i=4)
-                if on_vector(e0 + e):
-                    nc.vector.tensor_copy(dst, src)
-                else:
-                    nc.scalar.copy(dst, src)
+                round_w2(g[:, e * N * PACK : (e + 1) * N * PACK], raw[:, e, :], on_vector(e0 + e))
             cols = slice(e0 * N, e1 * N)
             nc.vector.quantize_mx(out=w2_words[:, cols].bitcast(FP8X4), scales=w2_scales[:, cols], in_=g[:])
 
@@ -167,16 +177,13 @@ def tile_moe_pkd_mlp_gelu_kernel(
         sums = None
         for e in range(E):
             raws = load_w1(e)
-            if e == 1:
-                for lst, pos in zip(token_slot, (pos1, pos2, pos3)):
-                    nc.sync.dma_start(lst[:], pos)
             if e % GATHER_EXPERTS == 0:
                 tokens = gather_tokens(e)
             grouped = round_w1(e, raws)
             previous = sums
             sums = first_layer(e, grouped, *tokens)
             if e > 0:
-                hidden(e - 1, previous, raws[0])
+                hidden(e - 1, previous, raws[1 if e == E - 1 else 0])
             if e in W2_EARLY:
                 e0, e1 = W2_EARLY[e]
                 quantize_w2(e0, e1, load_w2(e0, e1), lambda x: False)
@@ -185,28 +192,60 @@ def tile_moe_pkd_mlp_gelu_kernel(
                     second_layer(e0, e1)
         late = [load_w2(e0, e1) for e0, e1 in W2_LATE]
         gates = []
-        for r in range(TOP):
+        for r, pos in enumerate((pos1, pos2, pos3)):
+            nc.sync.dma_start(token_slot[r][:], pos)
             g = stream.tile([P, T], F32, name="gate", tag="stream", align_bytes=64)
             nc.sync.dma_start(g[:], gate[r])
             gates.append(g)
-        for (e0, e1), raw in zip(W2_LATE, late):
-            quantize_w2(e0, e1, raw, lambda x: x % 2 == 0)
-            if e1 == E - 1:
-                hidden(E - 1, sums, raw[:, 1, :])
+        e0, e1 = W2_LATE[0][0], E - 1
+        g = work.tile([P, (e1 - e0) * N * PACK], BF16, name="w2_bf16", align_bytes=64)
+        for e in range(e1 - e0):
+            round_w2(g[:, e * N * PACK : (e + 1) * N * PACK], late[e // 2][:, e % 2, :], e % 2 == 0)
+        cols = slice(e0 * N, e1 * N)
+        nc.vector.quantize_mx(out=w2_words[:, cols].bitcast(FP8X4), scales=w2_scales[:, cols], in_=g[:])
+        both = late[-2][:, 1, :].bitcast(BF16)
+        nc.scalar.activation(
+            both[:, N * PACK :].rearrange("p (c t) -> p c t", t=PACK), sums[:].rearrange("p t c -> p c t"), GELU
+        )
+        round_w2(both[:, : N * PACK], late[-1][:, 0, :], True)
+        last_words = keep.tile([P, N + C], U32, name="last_words", align_bytes=64)
+        last_scales = keep.tile([P, N + C], U8, name="last_scales", align_bytes=64)
+        nc.vector.quantize_mx(out=last_words[:].bitcast(FP8X4), scales=last_scales[:], in_=both)
         second_layer(W2_LATE[0][0], E - 1)
-        second_layer(E - 1, E)
+        acc = psum.tile([P, C], F32, name="acc")
+        nc.tensor.matmul_mx(
+            out=acc[:],
+            lhsT=last_words[:, :N].bitcast(FP8X4),
+            lhsT_scale=last_scales[:, :N],
+            rhs=last_words[:, N:].bitcast(FP8X4),
+            rhs_scale=last_scales[:, N:],
+            start=True,
+            stop=True,
+        )
+        nc.scalar.copy(y[:, (E - 1) * C :], acc[:])
 
         parts = [keep.tile([P, T], F32, name="part%d" % r) for r in range(TOP)]
         pair = keep.tile([P, T], F32, name="pair")
         total = keep.tile([P, T], F32, name="total")
-        for t0, t1 in zip(TOKEN_CUTS, TOKEN_CUTS[1:]):
-            for r in range(TOP):
-                nc.vector.tensor_tensor(
-                    parts[r][:, t0:t1],
-                    y[:].indirect(token_slot[r][:, t0 // STRIPE : t1 // STRIPE]),
-                    gates[r][:, t0:t1],
-                    MULT,
-                )
-            nc.vector.tensor_add(pair[:, t0:t1], parts[0][:, t0:t1], parts[1][:, t0:t1])
+
+        def fetch(r, t0, t1):
+            nc.vector.tensor_tensor(
+                parts[r][:, t0:t1],
+                y[:].indirect(token_slot[r][:, t0 // STRIPE : t1 // STRIPE]),
+                gates[r][:, t0:t1],
+                MULT,
+            )
+
+        def finish(t0, t1):
             nc.vector.tensor_add(total[:, t0:t1], pair[:, t0:t1], parts[2][:, t0:t1])
             nc.sync.dma_start(out[:, t0:t1], total[:, t0:t1])
+
+        for r in range(TOP):
+            fetch(r, 0, TOKEN_CUT)
+        nc.vector.tensor_add(pair[:, :TOKEN_CUT], parts[0][:, :TOKEN_CUT], parts[1][:, :TOKEN_CUT])
+        fetch(0, TOKEN_CUT, T)
+        finish(0, TOKEN_CUT)
+        fetch(1, TOKEN_CUT, T)
+        fetch(2, TOKEN_CUT, T)
+        nc.vector.tensor_add(pair[:, TOKEN_CUT:], parts[0][:, TOKEN_CUT:], parts[1][:, TOKEN_CUT:])
+        finish(TOKEN_CUT, T)

@@ -20,9 +20,15 @@ MULT = mybir.AluOpType.mult
 P = 128
 PACK = 4
 PASSES = K // (P * PACK)
+QUADRANTS = 4
+SCALE_ROWS = 4
 STRIPE = 16
+RUN = 4
+LAST = E - 1
+
 GATHER_EXPERTS = 3
 STREAM_BUFS = 7
+SPLIT_LOADS_FROM = E - 2
 W2_EARLY = {1: (0, 4), 5: (4, 8), 9: (8, 10)}
 W2_LATE = ((10, 12), (12, 14), (14, 15))
 VECTOR_SHARE = (52, 88)
@@ -41,57 +47,55 @@ def tile_moe_pkd_mlp_gelu_kernel(
 
         tok_scales = keep.tile([P, T], U8, name="tok_scales", align_bytes=64)
         nc.vector.memset(tok_scales[:].bitcast(I32), 0)
-        warm = keep.tile([P, 8], F32, name="warm")
-        warm_out = keep.tile([P, 8], F32, name="warm_out")
-        nc.vector.memset(warm[:], 0.0)
-        nc.scalar.activation(warm_out[:], warm[:], GELU)
-
         slot_token = keep.tile([P, S // STRIPE], U16, name="slot_token")
         tok_words = keep.tile([P, PASSES, T], I32, name="tok_words", align_bytes=64)
         nc.sync.dma_start(tok_words[:], x_words.rearrange("o p t r -> p o (t r)").bitcast(I32))
         nc.sync.dma_start(slot_token[:], offs)
-        for q in range(4):
+        for q in range(QUADRANTS):
             nc.sync.dma_start(
-                tok_scales[32 * q : 32 * q + 4 * PASSES, :].bitcast(I32),
-                x_scales[:, 4 * q : 4 * q + 4, :].bitcast(I32),
+                tok_scales[32 * q : 32 * q + SCALE_ROWS * PASSES, :].bitcast(I32),
+                x_scales[:, SCALE_ROWS * q : SCALE_ROWS * (q + 1), :].bitcast(I32),
             )
         token_slot = [keep.tile([P, T // STRIPE], U16, name="token_slot%d" % r) for r in range(TOP)]
 
-        h_words = keep.tile([P, S - C], U32, name="h_words", align_bytes=64)
-        h_scales = keep.tile([P, S - C], U8, name="h_scales", align_bytes=64)
-        w2_words = keep.tile([P, (E - 1) * N], U32, name="w2_words", align_bytes=64)
-        w2_scales = keep.tile([P, (E - 1) * N], U8, name="w2_scales", align_bytes=64)
+        h_words = keep.tile([P, LAST * C], U32, name="h_words", align_bytes=64)
+        h_scales = keep.tile([P, LAST * C], U8, name="h_scales", align_bytes=64)
+        w2_words = keep.tile([P, LAST * N], U32, name="w2_words", align_bytes=64)
+        w2_scales = keep.tile([P, LAST * N], U8, name="w2_scales", align_bytes=64)
         y = keep.tile([P, S], F32, name="y")
 
+        def quantize(words, scales, values):
+            nc.vector.quantize_mx(out=words.bitcast(FP8X4), scales=scales, in_=values)
+
         def gather_tokens(e0):
-            slots = slice(e0 * C, (e0 + GATHER_EXPERTS) * C)
-            offsets = slot_token[:, slots.start // STRIPE : slots.stop // STRIPE]
-            words = work.tile([P, PASSES, GATHER_EXPERTS * C], U32, name="slot_words", bufs=2, align_bytes=64)
-            scales = work.tile([P, GATHER_EXPERTS * C], U8, name="slot_scales", bufs=2, align_bytes=64)
+            width = GATHER_EXPERTS * C
+            offsets = slot_token[:, e0 * C // STRIPE : (e0 * C + width) // STRIPE]
+            words = work.tile([P, PASSES, width], U32, name="slot_words", bufs=2, align_bytes=64)
+            scales = work.tile([P, width], U8, name="slot_scales", bufs=2, align_bytes=64)
             for o in range(PASSES):
                 nc.vector.tensor_copy(words[:, o, :], tok_words[:, o, :].bitcast(U32).indirect(offsets))
             nc.vector.tensor_copy(scales[:], tok_scales[:].indirect(offsets))
             return words, scales
 
         def load_w1(e):
-            if e < E - 2:
-                raw = stream.tile([P, PASSES, PACK * H], F32, name="w1_raw", tag="stream", align_bytes=64)
-                nc.sync.dma_start(raw[:], w1[e].rearrange("(o p j) i -> p o (j i)", p=P, j=PACK))
-                return [raw[:, o, :] for o in range(PASSES)]
-            raws = []
+            if e < SPLIT_LOADS_FROM:
+                staged = stream.tile([P, PASSES, PACK * H], F32, name="w1_raw", tag="stream", align_bytes=64)
+                nc.sync.dma_start(staged[:], w1[e].rearrange("(o p j) i -> p o (j i)", p=P, j=PACK))
+                return [staged[:, o, :] for o in range(PASSES)]
+            views = []
             for o in range(PASSES):
-                raw = stream.tile([P, PACK * H], F32, name="w1_raw_pass", tag="stream", align_bytes=64)
-                nc.sync.dma_start(raw[:], w1[e].rearrange("(o p j) i -> o p (j i)", p=P, j=PACK)[o])
-                raws.append(raw[:])
-            return raws
+                staged = stream.tile([P, PACK * H], F32, name="w1_raw_pass", tag="stream", align_bytes=64)
+                nc.sync.dma_start(staged[:], w1[e].rearrange("(o p j) i -> o p (j i)", p=P, j=PACK)[o])
+                views.append(staged[:])
+            return views
 
-        def round_w1(e, raws):
-            grouped = []
-            for o, raw in enumerate(raws):
-                g = work.tile([P, PACK * H], BF16, name="w1_bf16_%d" % o, align_bytes=64)
-                dst = g[:].rearrange("p (t m j) -> p m j t", t=PACK, j=PACK)
-                src = raw.rearrange("p (j m t) -> p m j t", j=PACK, t=PACK)
-                if e == E - 1:
+        def round_w1(e, w1_staged):
+            rounded = []
+            for o, staged in enumerate(w1_staged):
+                values = work.tile([P, PACK * H], BF16, name="w1_bf16_%d" % o, align_bytes=64)
+                dst = values[:].rearrange("p (t m j) -> p m j t", t=PACK, j=PACK)
+                src = staged.rearrange("p (j m t) -> p m j t", j=PACK, t=PACK)
+                if e == LAST:
                     cut = VECTOR_SHARE[o]
                     nc.vector.tensor_copy(dst[:, :cut], src[:, :cut])
                     nc.scalar.copy(dst[:, cut:], src[:, cut:])
@@ -99,153 +103,153 @@ def tile_moe_pkd_mlp_gelu_kernel(
                     nc.scalar.copy(dst, src)
                 else:
                     nc.vector.tensor_copy(dst, src)
-                grouped.append(g)
-            return grouped
+                rounded.append(values)
+            return rounded
 
-        def first_layer(e, grouped, slot_words, slot_scales):
+        def first_layer(e, rounded, slot_words, slot_scales):
             slots = slice(e % GATHER_EXPERTS * C, (e % GATHER_EXPERTS + 1) * C)
-            codes = []
-            for o in reversed(range(PASSES)) if e < E - 2 else range(PASSES):
+            order = reversed(range(PASSES)) if e < SPLIT_LOADS_FROM else range(PASSES)
+            codes = {}
+            for o in order:
                 words = work.tile([P, H], U32, name="w1_words%d" % o, align_bytes=64)
                 scales = work.tile([P, H], U8, name="w1_scales%d" % o, align_bytes=64)
-                step = P if (e, o) == (E - 1, PASSES - 1) else H
-                for c in range(0, H, step):
-                    nc.vector.quantize_mx(
-                        out=words[:, c : c + step].bitcast(FP8X4),
-                        scales=scales[:, c : c + step],
-                        in_=grouped[o][:, PACK * c : PACK * (c + step)],
-                    )
-                codes.append((o, words, scales))
-            codes = sorted(codes, key=lambda item: item[0])
+                width = P if (e, o) == (LAST, PASSES - 1) else H
+                for c0 in range(0, H, width):
+                    c1 = c0 + width
+                    quantize(words[:, c0:c1], scales[:, c0:c1], rounded[o][:, PACK * c0 : PACK * c1])
+                codes[o] = (words, scales)
             a = psum.tile([P, PACK, C], F32, name="a")
             for t in range(PACK):
                 cols = slice(t * P, (t + 1) * P)
-                for o, words, scales in codes:
+                for o in range(PASSES):
+                    words, scales = codes[o]
                     nc.tensor.matmul_mx(
                         out=a[:, t, :],
                         lhsT=words[:, cols].bitcast(FP8X4),
                         lhsT_scale=scales[:, cols],
                         rhs=slot_words[:, o, slots].bitcast(FP8X4),
-                        rhs_scale=slot_scales[4 * o :, slots],
+                        rhs_scale=slot_scales[SCALE_ROWS * o :, slots],
                         start=(o == 0),
                         stop=(o == PASSES - 1),
                     )
             return a
 
+        def gelu(h, a):
+            nc.scalar.activation(h.rearrange("p (c t) -> p c t", t=PACK), a[:].rearrange("p t c -> p c t"), GELU)
+
         def hidden(e, a, spent):
             slots = slice(e * C, (e + 1) * C)
             h = spent[:, : C * PACK // 2].bitcast(BF16)
-            nc.scalar.activation(h.rearrange("p (c t) -> p c t", t=PACK), a[:].rearrange("p t c -> p c t"), GELU)
-            nc.vector.quantize_mx(out=h_words[:, slots].bitcast(FP8X4), scales=h_scales[:, slots], in_=h)
+            gelu(h, a)
+            quantize(h_words[:, slots], h_scales[:, slots], h)
 
         def load_w2(e0, e1):
-            raw = stream.tile([P, e1 - e0, PACK * N], F32, name="w2_raw", tag="stream", align_bytes=64)
-            nc.sync.dma_start(raw[:], w2[e0:e1].rearrange("e (p j) n -> p e (j n)", j=PACK))
-            return raw
+            staged = stream.tile([P, e1 - e0, PACK * N], F32, name="w2_raw", tag="stream", align_bytes=64)
+            nc.sync.dma_start(staged[:], w2[e0:e1].rearrange("e (p j) n -> p e (j n)", j=PACK))
+            return staged
 
-        def round_w2(grouped, raw, on_vector):
-            dst = grouped.rearrange("p (c i j) -> p c j i", i=4, j=PACK)
-            src = raw.rearrange("p (j c i) -> p c j i", j=PACK, i=4)
-            if on_vector:
-                nc.vector.tensor_copy(dst, src)
-            else:
-                nc.scalar.copy(dst, src)
+        def round_w2(copy, values, staged):
+            copy(
+                values.rearrange("p (c u j) -> p c j u", u=RUN, j=PACK),
+                staged.rearrange("p (j c u) -> p c j u", j=PACK, u=RUN),
+            )
 
-        def quantize_w2(e0, e1, raw, on_vector):
-            g = work.tile([P, (e1 - e0) * N * PACK], BF16, name="w2_bf16", align_bytes=64)
-            for e in range(e1 - e0):
-                round_w2(g[:, e * N * PACK : (e + 1) * N * PACK], raw[:, e, :], on_vector(e0 + e))
-            cols = slice(e0 * N, e1 * N)
-            nc.vector.quantize_mx(out=w2_words[:, cols].bitcast(FP8X4), scales=w2_scales[:, cols], in_=g[:])
+        def quantize_w2(e0, jobs):
+            values = work.tile([P, len(jobs) * N * PACK], BF16, name="w2_bf16", align_bytes=64)
+            for n_done, (copy, staged) in enumerate(jobs):
+                round_w2(copy, values[:, n_done * N * PACK : (n_done + 1) * N * PACK], staged)
+            cols = slice(e0 * N, (e0 + len(jobs)) * N)
+            quantize(w2_words[:, cols], w2_scales[:, cols], values[:])
 
-        def second_layer(e0, e1):
-            acc = psum.tile([P, (e1 - e0) * C], F32, name="acc")
-            for e in range(e0, e1):
-                cols = slice(e * N, (e + 1) * N)
-                slots = slice(e * C, (e + 1) * C)
+        def second_layer(e0, operands):
+            acc = psum.tile([P, len(operands) * C], F32, name="acc")
+            for n_done, (lhs_words, lhs_scales, rhs_words, rhs_scales) in enumerate(operands):
                 nc.tensor.matmul_mx(
-                    out=acc[:, (e - e0) * C : (e - e0 + 1) * C],
-                    lhsT=w2_words[:, cols].bitcast(FP8X4),
-                    lhsT_scale=w2_scales[:, cols],
-                    rhs=h_words[:, slots].bitcast(FP8X4),
-                    rhs_scale=h_scales[:, slots],
+                    out=acc[:, n_done * C : (n_done + 1) * C],
+                    lhsT=lhs_words.bitcast(FP8X4),
+                    lhsT_scale=lhs_scales,
+                    rhs=rhs_words.bitcast(FP8X4),
+                    rhs_scale=rhs_scales,
                     start=True,
                     stop=True,
                 )
-            nc.scalar.copy(y[:, e0 * C : e1 * C], acc[:])
+            nc.scalar.copy(y[:, e0 * C : (e0 + len(operands)) * C], acc[:])
+
+        def kept_operands(e0, e1):
+            return [
+                (
+                    w2_words[:, e * N : (e + 1) * N],
+                    w2_scales[:, e * N : (e + 1) * N],
+                    h_words[:, e * C : (e + 1) * C],
+                    h_scales[:, e * C : (e + 1) * C],
+                )
+                for e in range(e0, e1)
+            ]
 
         sums = None
         for e in range(E):
-            raws = load_w1(e)
+            w1_staged = load_w1(e)
             if e % GATHER_EXPERTS == 0:
                 tokens = gather_tokens(e)
-            grouped = round_w1(e, raws)
-            previous = sums
-            sums = first_layer(e, grouped, *tokens)
+            rounded = round_w1(e, w1_staged)
+            previous_sums = sums
+            sums = first_layer(e, rounded, *tokens)
             if e > 0:
-                hidden(e - 1, previous, raws[1 if e == E - 1 else 0])
+                hidden(e - 1, previous_sums, w1_staged[1 if e == LAST else 0])
             if e in W2_EARLY:
                 e0, e1 = W2_EARLY[e]
-                quantize_w2(e0, e1, load_w2(e0, e1), lambda x: False)
+                staged = load_w2(e0, e1)
+                quantize_w2(e0, [(nc.scalar.copy, staged[:, m, :]) for m in range(e1 - e0)])
             for e0, e1 in W2_EARLY.values():
                 if e == e1:
-                    second_layer(e0, e1)
-        late = [load_w2(e0, e1) for e0, e1 in W2_LATE]
+                    second_layer(e0, kept_operands(e0, e1))
+
+        *pairs, last_w2 = [load_w2(e0, e1) for e0, e1 in W2_LATE]
         gates = []
         for r, pos in enumerate((pos1, pos2, pos3)):
             nc.sync.dma_start(token_slot[r][:], pos)
-            g = stream.tile([P, T], F32, name="gate", tag="stream", align_bytes=64)
-            nc.sync.dma_start(g[:], gate[r])
-            gates.append(g)
-        e0, e1 = W2_LATE[0][0], E - 1
-        g = work.tile([P, (e1 - e0) * N * PACK], BF16, name="w2_bf16", align_bytes=64)
-        for e in range(e1 - e0):
-            round_w2(g[:, e * N * PACK : (e + 1) * N * PACK], late[e // 2][:, e % 2, :], e % 2 == 0)
-        cols = slice(e0 * N, e1 * N)
-        nc.vector.quantize_mx(out=w2_words[:, cols].bitcast(FP8X4), scales=w2_scales[:, cols], in_=g[:])
-        both = late[-2][:, 1, :].bitcast(BF16)
-        nc.scalar.activation(
-            both[:, N * PACK :].rearrange("p (c t) -> p c t", t=PACK), sums[:].rearrange("p t c -> p c t"), GELU
-        )
-        round_w2(both[:, : N * PACK], late[-1][:, 0, :], True)
+            gate_r = stream.tile([P, T], F32, name="gate", tag="stream", align_bytes=64)
+            nc.sync.dma_start(gate_r[:], gate[r])
+            gates.append(gate_r)
+
+        first_late = W2_LATE[0][0]
+        copies = (nc.vector.tensor_copy, nc.scalar.copy)
+        quantize_w2(first_late, [(copies[m], staged[:, m, :]) for staged in pairs for m in range(2)])
+
+        last_values = pairs[-1][:, 1, :].bitcast(BF16)
+        gelu(last_values[:, N * PACK :], sums)
+        round_w2(nc.vector.tensor_copy, last_values[:, : N * PACK], last_w2[:, 0, :])
         last_words = keep.tile([P, N + C], U32, name="last_words", align_bytes=64)
         last_scales = keep.tile([P, N + C], U8, name="last_scales", align_bytes=64)
-        nc.vector.quantize_mx(out=last_words[:].bitcast(FP8X4), scales=last_scales[:], in_=both)
-        second_layer(W2_LATE[0][0], E - 1)
-        acc = psum.tile([P, C], F32, name="acc")
-        nc.tensor.matmul_mx(
-            out=acc[:],
-            lhsT=last_words[:, :N].bitcast(FP8X4),
-            lhsT_scale=last_scales[:, :N],
-            rhs=last_words[:, N:].bitcast(FP8X4),
-            rhs_scale=last_scales[:, N:],
-            start=True,
-            stop=True,
-        )
-        nc.scalar.copy(y[:, (E - 1) * C :], acc[:])
+        quantize(last_words[:], last_scales[:], last_values)
+        second_layer(first_late, kept_operands(first_late, LAST))
+        second_layer(LAST, [(last_words[:, :N], last_scales[:, :N], last_words[:, N:], last_scales[:, N:])])
 
-        parts = [keep.tile([P, T], F32, name="part%d" % r) for r in range(TOP)]
-        pair = keep.tile([P, T], F32, name="pair")
+        products = [keep.tile([P, T], F32, name="part%d" % r) for r in range(TOP)]
+        first_two = keep.tile([P, T], F32, name="pair")
         total = keep.tile([P, T], F32, name="total")
 
         def fetch(r, t0, t1):
             nc.vector.tensor_tensor(
-                parts[r][:, t0:t1],
+                products[r][:, t0:t1],
                 y[:].indirect(token_slot[r][:, t0 // STRIPE : t1 // STRIPE]),
                 gates[r][:, t0:t1],
                 MULT,
             )
 
+        def add_first_two(t0, t1):
+            nc.vector.tensor_add(first_two[:, t0:t1], products[0][:, t0:t1], products[1][:, t0:t1])
+
         def finish(t0, t1):
-            nc.vector.tensor_add(total[:, t0:t1], pair[:, t0:t1], parts[2][:, t0:t1])
+            nc.vector.tensor_add(total[:, t0:t1], first_two[:, t0:t1], products[2][:, t0:t1])
             nc.sync.dma_start(out[:, t0:t1], total[:, t0:t1])
 
         for r in range(TOP):
             fetch(r, 0, TOKEN_CUT)
-        nc.vector.tensor_add(pair[:, :TOKEN_CUT], parts[0][:, :TOKEN_CUT], parts[1][:, :TOKEN_CUT])
+        add_first_two(0, TOKEN_CUT)
         fetch(0, TOKEN_CUT, T)
         finish(0, TOKEN_CUT)
         fetch(1, TOKEN_CUT, T)
         fetch(2, TOKEN_CUT, T)
-        nc.vector.tensor_add(pair[:, TOKEN_CUT:], parts[0][:, TOKEN_CUT:], parts[1][:, TOKEN_CUT:])
+        add_first_two(TOKEN_CUT, T)
         finish(TOKEN_CUT, T)

from contextlib import ExitStack

import concourse.mybir as mybir

K, T, E, C, H, N = 1024, 640, 15, 128, 512, 128
TOP = 3
S = E * C
FLOPS = 2 * S * (K * H + H * N)

F32 = mybir.dt.float32
BF16 = mybir.dt.bfloat16
I32 = mybir.dt.int32
U32 = mybir.dt.uint32
U16 = mybir.dt.uint16
U8 = mybir.dt.uint8
FP8X4 = mybir.dt.float8_e4m3fn_x4
GELU = mybir.ActivationFunctionType.Gelu_apprx_tanh
MULT = mybir.AluOpType.mult

P = 128
PACK = 4
PASSES = K // (P * PACK)
QUADRANTS = 4
SCALE_ROWS = 4
STRIPE = 16
RUN = 4
LAST = E - 1

GATHER_EXPERTS = 3
STREAM_BUFS = 7
SPLIT_LOADS_FROM = E - 2
W2_EARLY = {1: (0, 4), 5: (4, 8), 9: (8, 10)}
W2_LATE = ((10, 12), (12, 14), (14, 15))
VECTOR_SHARE = (52, 88)
TOKEN_CUT = 384


def tile_moe_pkd_mlp_gelu_kernel(
    tc, x_words, x_scales, w1, w2, gate, offs, pos1, pos2, pos3, out
):
    nc = tc.nc
    with ExitStack() as ctx:
        keep = ctx.enter_context(tc.tile_pool(name="keep", bufs=1))
        stream = ctx.enter_context(tc.tile_pool(name="stream", bufs=STREAM_BUFS))
        work = ctx.enter_context(tc.tile_pool(name="work", bufs=3))
        psum = ctx.enter_context(tc.psum_pool(name="psum", bufs=4))

        tok_scales = keep.tile([P, T], U8, name="tok_scales", align_bytes=64)
        nc.vector.memset(tok_scales[:].bitcast(I32), 0)
        slot_token = keep.tile([P, S // STRIPE], U16, name="slot_token")
        tok_words = keep.tile([P, PASSES, T], I32, name="tok_words", align_bytes=64)
        nc.sync.dma_start(tok_words[:], x_words.rearrange("o p t r -> p o (t r)").bitcast(I32))
        nc.sync.dma_start(slot_token[:], offs)
        for q in range(QUADRANTS):
            nc.sync.dma_start(
                tok_scales[32 * q : 32 * q + SCALE_ROWS * PASSES, :].bitcast(I32),
                x_scales[:, SCALE_ROWS * q : SCALE_ROWS * (q + 1), :].bitcast(I32),
            )
        token_slot = [keep.tile([P, T // STRIPE], U16, name="token_slot%d" % r) for r in range(TOP)]

        h_words = keep.tile([P, LAST * C], U32, name="h_words", align_bytes=64)
        h_scales = keep.tile([P, LAST * C], U8, name="h_scales", align_bytes=64)
        w2_words = keep.tile([P, LAST * N], U32, name="w2_words", align_bytes=64)
        w2_scales = keep.tile([P, LAST * N], U8, name="w2_scales", align_bytes=64)
        y = keep.tile([P, S], F32, name="y")

        def quantize(words, scales, values):
            nc.vector.quantize_mx(out=words.bitcast(FP8X4), scales=scales, in_=values)

        def gather_tokens(e0):
            width = GATHER_EXPERTS * C
            offsets = slot_token[:, e0 * C // STRIPE : (e0 * C + width) // STRIPE]
            words = work.tile([P, PASSES, width], U32, name="slot_words", bufs=2, align_bytes=64)
            scales = work.tile([P, width], U8, name="slot_scales", bufs=2, align_bytes=64)
            for o in range(PASSES):
                nc.vector.tensor_copy(words[:, o, :], tok_words[:, o, :].bitcast(U32).indirect(offsets))
            nc.vector.tensor_copy(scales[:], tok_scales[:].indirect(offsets))
            return words, scales

        def load_w1(e):
            if e < SPLIT_LOADS_FROM:
                staged = stream.tile([P, PASSES, PACK * H], F32, name="w1_raw", tag="stream", align_bytes=64)
                nc.sync.dma_start(staged[:], w1[e].rearrange("(o p j) i -> p o (j i)", p=P, j=PACK))
                return [staged[:, o, :] for o in range(PASSES)]
            views = []
            for o in range(PASSES):
                staged = stream.tile([P, PACK * H], F32, name="w1_raw_pass", tag="stream", align_bytes=64)
                nc.sync.dma_start(staged[:], w1[e].rearrange("(o p j) i -> o p (j i)", p=P, j=PACK)[o])
                views.append(staged[:])
            return views

        def round_w1(e, w1_staged):
            rounded = []
            for o, staged in enumerate(w1_staged):
                values = work.tile([P, PACK * H], BF16, name="w1_bf16_%d" % o, align_bytes=64)
                dst = values[:].rearrange("p (t m j) -> p m j t", t=PACK, j=PACK)
                src = staged.rearrange("p (j m t) -> p m j t", j=PACK, t=PACK)
                if e == LAST:
                    cut = VECTOR_SHARE[o]
                    nc.vector.tensor_copy(dst[:, :cut], src[:, :cut])
                    nc.scalar.copy(dst[:, cut:], src[:, cut:])
                elif o == 0:
                    nc.scalar.copy(dst, src)
                else:
                    nc.vector.tensor_copy(dst, src)
                rounded.append(values)
            return rounded

        def first_layer(e, rounded, slot_words, slot_scales):
            slots = slice(e % GATHER_EXPERTS * C, (e % GATHER_EXPERTS + 1) * C)
            order = reversed(range(PASSES)) if e < SPLIT_LOADS_FROM else range(PASSES)
            codes = {}
            for o in order:
                words = work.tile([P, H], U32, name="w1_words%d" % o, align_bytes=64)
                scales = work.tile([P, H], U8, name="w1_scales%d" % o, align_bytes=64)
                width = P if (e, o) == (LAST, PASSES - 1) else H
                for c0 in range(0, H, width):
                    c1 = c0 + width
                    quantize(words[:, c0:c1], scales[:, c0:c1], rounded[o][:, PACK * c0 : PACK * c1])
                codes[o] = (words, scales)
            a = psum.tile([P, PACK, C], F32, name="a")
            for t in range(PACK):
                cols = slice(t * P, (t + 1) * P)
                for o in range(PASSES):
                    words, scales = codes[o]
                    nc.tensor.matmul_mx(
                        out=a[:, t, :],
                        lhsT=words[:, cols].bitcast(FP8X4),
                        lhsT_scale=scales[:, cols],
                        rhs=slot_words[:, o, slots].bitcast(FP8X4),
                        rhs_scale=slot_scales[SCALE_ROWS * o :, slots],
                        start=(o == 0),
                        stop=(o == PASSES - 1),
                    )
            return a

        def gelu(h, a):
            nc.scalar.activation(h.rearrange("p (c t) -> p c t", t=PACK), a[:].rearrange("p t c -> p c t"), GELU)

        def hidden(e, a, spent):
            slots = slice(e * C, (e + 1) * C)
            h = spent[:, : C * PACK // 2].bitcast(BF16)
            gelu(h, a)
            quantize(h_words[:, slots], h_scales[:, slots], h)

        def load_w2(e0, e1):
            staged = stream.tile([P, e1 - e0, PACK * N], F32, name="w2_raw", tag="stream", align_bytes=64)
            nc.sync.dma_start(staged[:], w2[e0:e1].rearrange("e (p j) n -> p e (j n)", j=PACK))
            return staged

        def round_w2(copy, values, staged):
            copy(
                values.rearrange("p (c u j) -> p c j u", u=RUN, j=PACK),
                staged.rearrange("p (j c u) -> p c j u", j=PACK, u=RUN),
            )

        def quantize_w2(e0, jobs):
            values = work.tile([P, len(jobs) * N * PACK], BF16, name="w2_bf16", align_bytes=64)
            for n_done, (copy, staged) in enumerate(jobs):
                round_w2(copy, values[:, n_done * N * PACK : (n_done + 1) * N * PACK], staged)
            cols = slice(e0 * N, (e0 + len(jobs)) * N)
            quantize(w2_words[:, cols], w2_scales[:, cols], values[:])

        def second_layer(e0, operands):
            acc = psum.tile([P, len(operands) * C], F32, name="acc")
            for n_done, (lhs_words, lhs_scales, rhs_words, rhs_scales) in enumerate(operands):
                nc.tensor.matmul_mx(
                    out=acc[:, n_done * C : (n_done + 1) * C],
                    lhsT=lhs_words.bitcast(FP8X4),
                    lhsT_scale=lhs_scales,
                    rhs=rhs_words.bitcast(FP8X4),
                    rhs_scale=rhs_scales,
                    start=True,
                    stop=True,
                )
            nc.scalar.copy(y[:, e0 * C : (e0 + len(operands)) * C], acc[:])

        def kept_operands(e0, e1):
            return [
                (
                    w2_words[:, e * N : (e + 1) * N],
                    w2_scales[:, e * N : (e + 1) * N],
                    h_words[:, e * C : (e + 1) * C],
                    h_scales[:, e * C : (e + 1) * C],
                )
                for e in range(e0, e1)
            ]

        sums = None
        for e in range(E):
            w1_staged = load_w1(e)
            if e % GATHER_EXPERTS == 0:
                tokens = gather_tokens(e)
            rounded = round_w1(e, w1_staged)
            previous_sums = sums
            sums = first_layer(e, rounded, *tokens)
            if e > 0:
                hidden(e - 1, previous_sums, w1_staged[1 if e == LAST else 0])
            if e in W2_EARLY:
                e0, e1 = W2_EARLY[e]
                staged = load_w2(e0, e1)
                quantize_w2(e0, [(nc.scalar.copy, staged[:, m, :]) for m in range(e1 - e0)])
            for e0, e1 in W2_EARLY.values():
                if e == e1:
                    second_layer(e0, kept_operands(e0, e1))

        *pairs, last_w2 = [load_w2(e0, e1) for e0, e1 in W2_LATE]
        gates = []
        for r, pos in enumerate((pos1, pos2, pos3)):
            nc.sync.dma_start(token_slot[r][:], pos)
            gate_r = stream.tile([P, T], F32, name="gate", tag="stream", align_bytes=64)
            nc.sync.dma_start(gate_r[:], gate[r])
            gates.append(gate_r)

        first_late = W2_LATE[0][0]
        copies = (nc.vector.tensor_copy, nc.scalar.copy)
        quantize_w2(first_late, [(copies[m], staged[:, m, :]) for staged in pairs for m in range(2)])

        last_values = pairs[-1][:, 1, :].bitcast(BF16)
        gelu(last_values[:, N * PACK :], sums)
        round_w2(nc.vector.tensor_copy, last_values[:, : N * PACK], last_w2[:, 0, :])
        last_words = keep.tile([P, N + C], U32, name="last_words", align_bytes=64)
        last_scales = keep.tile([P, N + C], U8, name="last_scales", align_bytes=64)
        quantize(last_words[:], last_scales[:], last_values)
        second_layer(first_late, kept_operands(first_late, LAST))
        second_layer(LAST, [(last_words[:, :N], last_scales[:, :N], last_words[:, N:], last_scales[:, N:])])

        products = [keep.tile([P, T], F32, name="part%d" % r) for r in range(TOP)]
        first_two = keep.tile([P, T], F32, name="pair")
        total = keep.tile([P, T], F32, name="total")

        def fetch(r, t0, t1):
            nc.vector.tensor_tensor(
                products[r][:, t0:t1],
                y[:].indirect(token_slot[r][:, t0 // STRIPE : t1 // STRIPE]),
                gates[r][:, t0:t1],
                MULT,
            )

        def add_first_two(t0, t1):
            nc.vector.tensor_add(first_two[:, t0:t1], products[0][:, t0:t1], products[1][:, t0:t1])

        def finish(t0, t1):
            nc.vector.tensor_add(total[:, t0:t1], first_two[:, t0:t1], products[2][:, t0:t1])
            nc.sync.dma_start(out[:, t0:t1], total[:, t0:t1])

        for r in range(TOP):
            fetch(r, 0, TOKEN_CUT)
        add_first_two(0, TOKEN_CUT)
        fetch(0, TOKEN_CUT, T)
        finish(0, TOKEN_CUT)
        fetch(1, TOKEN_CUT, T)
        fetch(2, TOKEN_CUT, T)
        add_first_two(TOKEN_CUT, T)
        finish(TOKEN_CUT, T)
